import numpy as np
import ml_dtypes


def mxq(x, axis, fmt="e4m3"):
    dtype, down = {"e4m3": (ml_dtypes.float8_e4m3fn, 7), "e5m2": (ml_dtypes.float8_e5m2, 14)}[fmt]
    v = np.moveaxis(np.asarray(x, np.float32).astype(ml_dtypes.bfloat16).astype(np.float64), axis, -1)
    blocks = v.reshape(v.shape[:-1] + (-1, 32))
    amax = np.abs(blocks).max(-1, keepdims=True)
    byte = np.maximum(np.where(amax > 0, np.frexp(amax)[1] - 1 + 127, 0) - down, 1)
    scale = np.exp2(byte - 127.0)
    codes = (blocks / scale).astype(np.float32).astype(dtype).astype(np.float64)
    return np.moveaxis((codes * scale).reshape(v.shape), -1, axis)


WIDE = False


def mx_kscale(k):
    if not WIDE:
        return np.ones(k)
    levels = np.array([10, -10, 5, -5, 0])
    if k % 512:
        return np.exp2(np.random.permutation(np.resize(levels, k // 32))).repeat(32)
    a = np.empty((k // 512, 16))
    for p in range(k // 512):
        a[p, :8] = np.random.permutation(np.resize(levels, 8))
        for g in range(8):
            far = levels[np.abs(levels - a[p, g]) >= 10]
            a[p, g + 8] = far[np.random.randint(len(far))]
    return np.exp2(a.ravel()).repeat(32)


def f64(x):
    return np.asarray(x).astype(np.float64)


def striped(idx):
    return np.tile(idx.reshape(-1, 16).T, (8, 1)).astype(np.uint16)


def unstriped(offs):
    return offs[:16].T.reshape(-1).astype(np.int64)


E2M1 = np.array([0.0, 0.5, 1.0, 1.5, 2.0, 3.0, 4.0, 6.0, -0.0, -0.5, -1.0, -1.5, -2.0, -3.0, -4.0, -6.0])


def pack_weight(w, fmt):
    k, n = w.shape
    w = f64(np.asarray(w, np.float32).astype(ml_dtypes.bfloat16)).reshape(k // 32, 32, n)
    amax = np.abs(w).max(1)
    if fmt == "e4m3":
        byte = np.frexp(amax)[1] - 1 + 127 - 7
    else:
        mant, ex = np.frexp(amax / 6.0)
        byte = np.where(mant > 0.5, ex, ex - 1) + 127
    byte = np.clip(np.where(amax > 0, byte, 1), 1, 254)
    scaled = (w * np.exp2(127.0 - byte)[:, None, :]).reshape(k, n).astype(np.float32)
    by_word = np.ascontiguousarray(scaled.reshape(k // 512, 128, 4, n).transpose(0, 1, 3, 2))
    if fmt == "e4m3":
        words = by_word.astype(ml_dtypes.float8_e4m3fn).view(np.uint8)
    else:
        c = by_word.astype(ml_dtypes.float4_e2m1fn).view(np.uint8) & 0xF
        words = (c[..., 0::2] | (c[..., 1::2] << 4)).reshape(k // 512, 128, 2 * n)
    return np.ascontiguousarray(words), np.ascontiguousarray(byte.astype(np.uint8).reshape(k // 512, 16, n))


def unpack_weight(words, scales, fmt):
    g, _, n = scales.shape
    words = np.ascontiguousarray(words).reshape(g, 128, n, -1)
    if fmt == "e4m3":
        vals = words.view(ml_dtypes.float8_e4m3fn).astype(np.float64)
    else:
        nib = np.empty((g, 128, n, 4), np.uint8)
        nib[..., 0::2] = words & 0xF
        nib[..., 1::2] = words >> 4
        vals = E2M1[nib]
    vals = vals * np.repeat(np.exp2(scales.astype(np.float64) - 127.0), 8, axis=1)[..., None]
    return vals.transpose(0, 1, 3, 2).reshape(g * 512, n)


def gelu(v):
    return 0.5 * v * (1.0 + np.tanh(np.sqrt(2.0 / np.pi) * (v + 0.044715 * v**3)))


K, T, S, H = 1536, 2048, 512, 1024

def setup_inputs():
    n = np.random.standard_normal
    s = mx_kscale(K)[:, None]
    u = mx_kscale(H)[:, None]
    tab_words, tab_scales = pack_weight(n((K, T)) * s, "e2m1")
    w2_words, w2_scales = pack_weight(n((K, H)) * u.T / s / np.sqrt(K), "e4m3")
    w4_words, w4_scales = pack_weight(1.5 * n((H, H)) / u / np.sqrt(H), "e2m1")
    return {
        "tab_words": tab_words, "tab_scales": tab_scales,
        "offs": striped(np.random.permutation(T)[:S]),
        "offs2": striped(np.random.permutation(T)[:S]),
        "w1": (n((K, H)) / s / np.sqrt(K)).astype(np.float32),
        "w2_words": w2_words, "w2_scales": w2_scales,
        "w3": (1.5 * n((H, H)) / u / np.sqrt(H)).astype(np.float32),
        "w4_words": w4_words, "w4_scales": w4_scales,
    }

def reference(tab_words, tab_scales, offs, offs2, w1, w2_words, w2_scales, w3, w4_words, w4_scales):
    TW = unpack_weight(tab_words, tab_scales, "e2m1")
    v = TW[:, unstriped(offs)]
    v2 = TW[:, unstriped(offs2)]
    w2 = unpack_weight(w2_words, w2_scales, "e4m3")
    w4 = unpack_weight(w4_words, w4_scales, "e2m1")
    p = mxq(f64(w1), 0, "e4m3").T @ v
    b = w2.T @ v2
    h = p / (1.0 + np.exp(-p)) * b
    hq = mxq(h, 0, "e4m3")
    d = mxq(f64(w3), 0, "e4m3").T @ hq
    e = np.tanh(d + p)
    return e + (w4.T @ hq)

@@ -1,0 +1,254 @@
+from contextlib import ExitStack
+
+import concourse.mybir as mybir
+
+K, T, S, H = 1536, 2048, 512, 1024
+FLOPS = 2 * S * H * (2 * K + 2 * H)
+
+F32 = mybir.dt.float32
+BF16 = mybir.dt.bfloat16
+I32 = mybir.dt.int32
+U32 = mybir.dt.uint32
+U16 = mybir.dt.uint16
+U8 = mybir.dt.uint8
+FP8X4 = mybir.dt.float8_e4m3fn_x4
+FP4X4 = mybir.dt.float4_e2m1fn_x4
+ACT = mybir.ActivationFunctionType
+ALU = mybir.AluOpType
+
+P = 128
+PACK = 4
+SPAN = P * PACK
+KP = K // SPAN
+HP = H // SPAN
+CHUNK = 128
+CHUNKS = S // CHUNK
+LIVE = 100
+
+
+def tile_list_syndicate_pair_features_kernel(
+    tc, tab_words, tab_scales, offs, offs2, w1, w2_words, w2_scales, w3, w4_words, w4_scales, out
+):
+    nc = tc.nc
+    with ExitStack() as ctx:
+        keep = ctx.enter_context(tc.tile_pool(name="keep", bufs=1))
+        raws = ctx.enter_context(tc.tile_pool(name="raws", bufs=4))
+        stage = ctx.enter_context(tc.tile_pool(name="stage", bufs=4))
+        psum = ctx.enter_context(tc.psum_pool(name="psum", bufs=1))
+
+        lists = [keep.tile([P, S // 16], U16, name=f"list{i}") for i in range(2)]
+        tab_planes = keep.tile([P, T], U8, align_bytes=64)
+        w_planes = keep.tile([P, H], U8, align_bytes=64)
+        v_moved = [keep.tile([P, 2, S], U8, align_bytes=64, name=f"v_moved{i}") for i in range(KP - 1)]
+        w_moved = [keep.tile([P, H], U8, align_bytes=64, name=f"w_moved{i}") for i in range(KP + HP - 1)]
+        for tile in [tab_planes, w_planes, *w_moved]:
+            nc.vector.memset(tile[:].bitcast(I32), 0)
+        for tile in v_moved:
+            nc.vector.memset(tile[:].rearrange("p l s -> p (l s)").bitcast(I32), 0)
+
+        def load_planes(tile, first, scales):
+            rows = 4 * scales.shape[0]
+            for q in range(4):
+                nc.sync.dma_start(
+                    out=tile[32 * q + first : 32 * q + first + rows, :].bitcast(I32),
+                    in_=scales[:, 4 * q : 4 * q + 4, :].bitcast(I32),
+                )
+
+        def load_float(w, a, g):
+            raw = raws.tile([P, PACK, SPAN], F32, name="raw")
+            rows = w[SPAN * a : SPAN * (a + 1), SPAN * g : SPAN * (g + 1)]
+            nc.sync.dma_start(out=raw[:], in_=rows.rearrange("(p j) c -> p j c", j=PACK))
+            return raw
+
+        def load_w2(g):
+            words = keep.tile([P, KP, SPAN], I32, name=f"packed_raw{g}")
+            cols = w2_words[:, :, SPAN * g : SPAN * (g + 1), :]
+            nc.sync.dma_start(out=words[:], in_=cols.rearrange("a p c i -> p a (c i)").bitcast(I32))
+            return words
+
+        tab = [keep.tile([P, T], U16, name=f"tab{a}") for a in range(KP)]
+        w1_raw, w2_raw, w3_raw = {}, {}, {}
+
+        def load_tab(a):
+            nc.sync.dma_start(out=tab[a][:].bitcast(I32), in_=tab_words[a].bitcast(I32))
+
+        nc.sync.dma_start(lists[0][:], offs)
+        load_tab(0)
+        load_planes(tab_planes, 0, tab_scales)
+        nc.sync.dma_start(lists[1][:], offs2)
+        w1_raw[0, 0] = load_float(w1, 0, 0)
+        load_tab(1)
+        load_planes(w_planes, 0, w2_scales)
+        w1_raw[1, 0] = load_float(w1, 1, 0)
+        load_tab(2)
+        load_planes(w_planes, 4 * KP, w4_scales)
+        w1_raw[2, 0] = load_float(w1, 2, 0)
+        w2_raw[0] = load_w2(0)
+        w1_raw[0, 1] = load_float(w1, 0, 1)
+        w2_raw[1] = load_w2(1)
+
+        def round_weight(raw, on_vector):
+            rounded = stage.tile([P, PACK * SPAN], BF16, align_bytes=64, name="rounded")
+            dst = rounded[:].rearrange("p (t m j) -> p m j t", t=PACK, j=PACK)
+            src = raw[:].rearrange("p j (m t) -> p m j t", t=PACK)
+            if on_vector:
+                nc.vector.tensor_copy(out=dst, in_=src)
+            else:
+                nc.scalar.copy(out=dst, in_=src)
+            return rounded
+
+        def quantise(values, name):
+            codes = keep.tile([P, SPAN], U32, align_bytes=64, name=f"{name}_codes")
+            scales = keep.tile([P, SPAN], U8, align_bytes=64, name=f"{name}_scales")
+            nc.vector.quantize_mx(out=codes[:].bitcast(FP8X4), scales=scales[:], in_=values[:])
+            return codes, scales
+
+        v_planes = keep.tile([P, 2, S], U8, align_bytes=64)
+        for side in range(2):
+            nc.vector.tensor_copy(v_planes[:, side, :], tab_planes[:].indirect(lists[side][:]))
+        for a in range(1, KP):
+            nc.gpsimd.dma_start(
+                out=v_moved[a - 1][0:LIVE, :, :].rearrange("p l s -> p (l s)").bitcast(I32),
+                in_=v_planes[4 * a : 4 * a + LIVE, :, :].rearrange("p l s -> p (l s)").bitcast(I32),
+            )
+        v_scales = [v_planes, *v_moved]
+
+        v_words = {}
+
+        def gather_words(side, a):
+            words = keep.tile([P, S], U16, align_bytes=64, name=f"v_words{side}{a}")
+            nc.vector.tensor_copy(words[:], tab[a][:].indirect(lists[side][:]))
+            v_words[side, a] = words
+
+        w1_q = {}
+        gather_words(0, 0)
+        gather_words(1, 0)
+        w1_q[0, 0] = quantise(round_weight(w1_raw[0, 0], False), "w1_00")
+
+        w_sorted = keep.tile([P, H], U8, align_bytes=64)
+        nc.vector.tensor_copy(
+            out=w_sorted[:].rearrange("p (g t m i) -> p g m t i", g=HP, t=PACK, i=16),
+            in_=w_planes[:].rearrange("p (g m i t) -> p g m t i", g=HP, t=PACK, i=16),
+        )
+        for n in range(1, KP + HP):
+            nc.gpsimd.dma_start(out=w_moved[n - 1][0:LIVE, :].bitcast(I32), in_=w_sorted[4 * n : 4 * n + LIVE, :].bitcast(I32))
+        w_scales = [w_sorted, *w_moved]
+
+        for a in range(1, KP):
+            gather_words(0, a)
+            gather_words(1, a)
+            w1_q[a, 0] = quantise(round_weight(w1_raw[a, 0], False), f"w1_{a}0")
+
+        w1_raw[1, 1] = load_float(w1, 1, 1)
+        w1_raw[2, 1] = load_float(w1, 2, 1)
+        w3_raw[0, 0] = load_float(w3, 0, 0)
+
+        def sort_w2(g):
+            words = keep.tile([P, KP, SPAN], I32, align_bytes=64, name=f"w2_sorted{g}")
+            nc.vector.tensor_copy(
+                out=words[:].rearrange("p a (t m i) -> p a m t i", t=PACK, i=4),
+                in_=w2_raw[g][:].rearrange("p a (m i t) -> p a m t i", t=PACK, i=4),
+            )
+            return words
+
+        def first_product(tag, side, weight):
+            banks = [psum.tile([P, PACK, CHUNK], F32, name=f"{tag}{c}") for c in range(CHUNKS)]
+            for a in range(KP):
+                for c in range(CHUNKS):
+                    cols = slice(CHUNK * c, CHUNK * (c + 1))
+                    for t in range(PACK):
+                        codes, scales = weight(a, t)
+                        nc.tensor.matmul_mx(
+                            out=banks[c][:, t, :],
+                            lhsT=codes.bitcast(FP8X4),
+                            lhsT_scale=scales,
+                            rhs=v_words[side, a][:, cols].bitcast(FP4X4),
+                            rhs_scale=v_scales[a][:, side, cols],
+                            start=(a == 0 and t == 0),
+                            stop=(a == KP - 1 and t == PACK - 1),
+                        )
+            return banks
+
+        h_q, lead = [], []
+        for g in range(HP):
+            w2_sorted = sort_w2(g)
+            if g == 0:
+                w4_raw = keep.tile([P, HP, H], U16, name="packed_raw0")
+                nc.sync.dma_start(out=w4_raw[:].bitcast(I32), in_=w4_words.rearrange("a p x -> p a x").bitcast(I32))
+            if g == 1:
+                for a in range(KP):
+                    w1_q[a, 1] = quantise(round_weight(w1_raw[a, 1], a > 0), f"w1_{a}1")
+                w3_raw[1, 0] = load_float(w3, 1, 0)
+                w3_raw[0, 1] = load_float(w3, 0, 1)
+                w3_raw[1, 1] = load_float(w3, 1, 1)
+
+            def w1_block(a, t):
+                codes, scales = w1_q[a, g]
+                return codes[:, P * t : P * (t + 1)], scales[:, P * t : P * (t + 1)]
+
+            def w2_block(a, t):
+                first = SPAN * g + P * t
+                return w2_sorted[:, a, P * t : P * (t + 1)], w_scales[a][:, first : first + P]
+
+            if g == 0:
+                p_banks = first_product("left", 0, w1_block)
+                b_banks = first_product("right", 1, w2_block)
+            else:
+                b_banks = first_product("right", 1, w2_block)
+                p_banks = first_product("left", 0, w1_block)
+            h = keep.tile([P, PACK * S], BF16, align_bytes=64, name=f"h{g}")
+            p_rows = keep.tile([P, PACK, S], F32, name=f"p_rows{g}")
+            for c in range(CHUNKS):
+                gate = stage.tile([P, CHUNK, PACK], F32, name="gate")
+                nc.scalar.activation(out=gate[:], in_=p_banks[c][:].rearrange("p t n -> p n t"), func=ACT.Silu)
+                nc.vector.tensor_tensor(
+                    out=h[:, SPAN * c : SPAN * (c + 1)].rearrange("p (n t) -> p n t", t=PACK),
+                    in0=b_banks[c][:].rearrange("p t n -> p n t"),
+                    in1=gate[:],
+                    op=ALU.mult,
+                )
+            for c in range(CHUNKS):
+                nc.scalar.copy(out=p_rows[:, :, CHUNK * c : CHUNK * (c + 1)], in_=p_banks[c][:])
+            h_q.append(quantise(h, f"h{g}"))
+            lead.append(p_rows)
+            if g == 0:
+                w4_sorted = keep.tile([P, HP, H], U16, align_bytes=64)
+                nc.vector.tensor_copy(
+                    out=w4_sorted[:].rearrange("p a (g t m i) -> p (a g) m t i", g=HP, t=PACK, i=8),
+                    in_=w4_raw[:].rearrange("p a (g m i t) -> p (a g) m t i", g=HP, t=PACK, i=8),
+                )
+
+        for g in range(HP):
+            w3_q = [quantise(round_weight(w3_raw[a, g], g == 0 and a == 0), f"w3_{a}{g}") for a in range(HP)]
+            rows = out[SPAN * g : SPAN * (g + 1), :].rearrange("(p t) j -> p t j", t=PACK)
+            for t in range(PACK):
+                first = SPAN * g + P * t
+                y_bank = psum.tile([P, S], F32, name=f"right{t}")
+                d_bank = psum.tile([P, S], F32, name=f"left{t}")
+                for a in range(HP):
+                    nc.tensor.matmul_mx(
+                        out=y_bank[:],
+                        lhsT=w4_sorted[:, a, first : first + P].bitcast(FP4X4),
+                        lhsT_scale=w_scales[KP + a][:, first : first + P],
+                        rhs=h_q[a][0][:].bitcast(FP8X4),
+                        rhs_scale=h_q[a][1][:],
+                        start=(a == 0),
+                        stop=(a == HP - 1),
+                    )
+                for a in range(HP):
+                    nc.tensor.matmul_mx(
+                        out=d_bank[:],
+                        lhsT=w3_q[a][0][:, P * t : P * (t + 1)].bitcast(FP8X4),
+                        lhsT_scale=w3_q[a][1][:, P * t : P * (t + 1)],
+                        rhs=h_q[a][0][:].bitcast(FP8X4),
+                        rhs_scale=h_q[a][1][:],
+                        start=(a == 0),
+                        stop=(a == HP - 1),
+                    )
+                inner = stage.tile([P, S], F32, name="inner")
+                nc.vector.tensor_tensor(out=inner[:], in0=d_bank[:], in1=lead[g][:, t, :], op=ALU.add)
+                squashed = stage.tile([P, S], F32, name="squashed")
+                nc.scalar.activation(out=squashed[:], in_=inner[:], func=ACT.Tanh)
+                result = stage.tile([P, S], F32, name="result")
+                nc.vector.tensor_tensor(out=result[:], in0=y_bank[:], in1=squashed[:], op=ALU.add)
+                nc.sync.dma_start(out=rows[:, t, :], in_=result[:])

@@ -24,6 +24,10 @@ HP = H // SPAN
 CHUNK = 128
 CHUNKS = S // CHUNK
 LIVE = 100
+AGAIN = 2
+AG = 1
+WEAVE = False
+C20, C11, C21, D00, D10, D01, D11 = 0, 0, 4, 0, 4, 0, 0
 
 
 def tile_list_syndicate_pair_features_kernel(
@@ -32,69 +36,81 @@ def tile_list_syndicate_pair_features_kernel(
     nc = tc.nc
     with ExitStack() as ctx:
         keep = ctx.enter_context(tc.tile_pool(name="keep", bufs=1))
-        raws = ctx.enter_context(tc.tile_pool(name="raws", bufs=4))
         stage = ctx.enter_context(tc.tile_pool(name="stage", bufs=4))
         psum = ctx.enter_context(tc.psum_pool(name="psum", bufs=1))
 
         lists = [keep.tile([P, S // 16], U16, name=f"list{i}") for i in range(2)]
-        tab_planes = keep.tile([P, T], U8, align_bytes=64)
-        w_planes = keep.tile([P, H], U8, align_bytes=64)
+        tab_planes = keep.tile([P, T], U8, align_bytes=64, name="raw2")
+        w2_planes = keep.tile([P, KP, H], U8, align_bytes=64)
         v_moved = [keep.tile([P, 2, S], U8, align_bytes=64, name=f"v_moved{i}") for i in range(KP - 1)]
-        w_moved = [keep.tile([P, H], U8, align_bytes=64, name=f"w_moved{i}") for i in range(KP + HP - 1)]
-        for tile in [tab_planes, w_planes, *w_moved]:
-            nc.vector.memset(tile[:].bitcast(I32), 0)
-        for tile in v_moved:
-            nc.vector.memset(tile[:].rearrange("p l s -> p (l s)").bitcast(I32), 0)
 
-        def load_planes(tile, first, scales):
+        def load_packed_planes(queue, tile, scales):
             rows = 4 * scales.shape[0]
             for q in range(4):
-                nc.sync.dma_start(
-                    out=tile[32 * q + first : 32 * q + first + rows, :].bitcast(I32),
+                queue.dma_start(
+                    out=tile[32 * q : 32 * q + rows, :].bitcast(I32),
                     in_=scales[:, 4 * q : 4 * q + 4, :].bitcast(I32),
                 )
 
-        def load_float(w, a, g):
-            raw = raws.tile([P, PACK, SPAN], F32, name="raw")
+        def load_planes(queue, tile, scales):
+            for q in range(4):
+                queue.dma_start(
+                    out=tile[32 * q : 32 * q + 4, :, :].bitcast(I32),
+                    in_=scales[:, 4 * q : 4 * q + 4, :].rearrange("a r c -> r a c").bitcast(I32),
+                )
+
+        nc.gpsimd.memset(tab_planes[:].bitcast(I32), 0)
+        for tile in [w2_planes, *v_moved]:
+            nc.vector.memset(tile[:].rearrange("p a c -> p (a c)").bitcast(I32), 0)
+        w4_planes = keep.tile([P, 1, H], U8, align_bytes=64)
+        w4_moved = keep.tile([P, H], U8, align_bytes=64)
+        for tile in [w4_planes[:, 0, :], w4_moved[:]]:
+            nc.vector.memset(tile.bitcast(I32), 0)
+        load_packed_planes(nc.gpsimd, w4_planes[:, 0, :], w4_scales)
+        warm = keep.tile([P, 2], F32)
+        nc.vector.memset(warm[:], 0.0)
+        nc.scalar.activation(out=warm[:, 1:2], in_=warm[:, 0:1], func=ACT.Silu)
+
+        def load_float(w, a, g, slot):
+            raw = keep.tile([P, PACK, SPAN], F32, align_bytes=64, name=slot)
             rows = w[SPAN * a : SPAN * (a + 1), SPAN * g : SPAN * (g + 1)]
             nc.sync.dma_start(out=raw[:], in_=rows.rearrange("(p j) c -> p j c", j=PACK))
             return raw
 
-        def load_w2(g):
-            words = keep.tile([P, KP, SPAN], I32, name=f"packed_raw{g}")
+        def load_w2(g, slot):
+            words = keep.tile([P, KP, SPAN], I32, align_bytes=64, name=slot)
             cols = w2_words[:, :, SPAN * g : SPAN * (g + 1), :]
             nc.sync.dma_start(out=words[:], in_=cols.rearrange("a p c i -> p a (c i)").bitcast(I32))
             return words
 
-        tab = [keep.tile([P, T], U16, name=f"tab{a}") for a in range(KP)]
+        tab = [keep.tile([P, T], U16, align_bytes=64, name=f"tab{a}") for a in range(KP)]
         w1_raw, w2_raw, w3_raw = {}, {}, {}
 
         def load_tab(a):
             nc.sync.dma_start(out=tab[a][:].bitcast(I32), in_=tab_words[a].bitcast(I32))
 
         nc.sync.dma_start(lists[0][:], offs)
-        load_tab(0)
-        load_planes(tab_planes, 0, tab_scales)
         nc.sync.dma_start(lists[1][:], offs2)
-        w1_raw[0, 0] = load_float(w1, 0, 0)
+        load_tab(0)
+        w1_raw[0, 0] = load_float(w1, 0, 0, "raw0")
+        load_packed_planes(nc.sync, tab_planes, tab_scales)
+        w2_raw[0] = load_w2(0, "w2_raw")
         load_tab(1)
-        load_planes(w_planes, 0, w2_scales)
-        w1_raw[1, 0] = load_float(w1, 1, 0)
+        load_planes(nc.sync, w2_planes, w2_scales)
+        w1_raw[1, 0] = load_float(w1, 1, 0, "raw1")
         load_tab(2)
-        load_planes(w_planes, 4 * KP, w4_scales)
-        w1_raw[2, 0] = load_float(w1, 2, 0)
-        w2_raw[0] = load_w2(0)
-        w1_raw[0, 1] = load_float(w1, 0, 1)
-        w2_raw[1] = load_w2(1)
 
-        def round_weight(raw, on_vector):
-            rounded = stage.tile([P, PACK * SPAN], BF16, align_bytes=64, name="rounded")
+        def round_weight(raw, on_vector, slot=None):
+            if slot is None:
+                rounded = stage.tile([P, PACK * SPAN], BF16, align_bytes=64, name="rounded")
+            else:
+                rounded = keep.tile([P, PACK * SPAN], BF16, align_bytes=64, name=slot)
             dst = rounded[:].rearrange("p (t m j) -> p m j t", t=PACK, j=PACK)
             src = raw[:].rearrange("p j (m t) -> p m j t", t=PACK)
-            if on_vector:
-                nc.vector.tensor_copy(out=dst, in_=src)
-            else:
-                nc.scalar.copy(out=dst, in_=src)
+            if on_vector > 0:
+                nc.vector.tensor_copy(out=dst[:, :, :, 0:on_vector], in_=src[:, :, :, 0:on_vector])
+            if on_vector < PACK:
+                nc.scalar.copy(out=dst[:, :, :, on_vector:PACK], in_=src[:, :, :, on_vector:PACK])
             return rounded
 
         def quantise(values, name):
@@ -103,58 +119,72 @@ def tile_list_syndicate_pair_features_kernel(
             nc.vector.quantize_mx(out=codes[:].bitcast(FP8X4), scales=scales[:], in_=values[:])
             return codes, scales
 
-        v_planes = keep.tile([P, 2, S], U8, align_bytes=64)
-        for side in range(2):
-            nc.vector.tensor_copy(v_planes[:, side, :], tab_planes[:].indirect(lists[side][:]))
-        for a in range(1, KP):
-            nc.gpsimd.dma_start(
-                out=v_moved[a - 1][0:LIVE, :, :].rearrange("p l s -> p (l s)").bitcast(I32),
-                in_=v_planes[4 * a : 4 * a + LIVE, :, :].rearrange("p l s -> p (l s)").bitcast(I32),
-            )
-        v_scales = [v_planes, *v_moved]
-
         v_words = {}
 
         def gather_words(side, a):
-            words = keep.tile([P, S], U16, align_bytes=64, name=f"v_words{side}{a}")
+            slot = f"first{a - 1}" if side == 0 and a > 0 else f"v_words{side}{a}"
+            words = keep.tile([P, S], U16, align_bytes=64, name=slot)
             nc.vector.tensor_copy(words[:], tab[a][:].indirect(lists[side][:]))
             v_words[side, a] = words
 
-        w1_q = {}
+        def sort_planes(planes, g, name):
+            passes = planes.shape[1]
+            ordered = keep.tile([P, passes, SPAN], U8, align_bytes=64, name=name)
+            nc.vector.tensor_copy(
+                out=ordered[:].rearrange("p a (t m i) -> p m a t i", t=PACK, i=16),
+                in_=planes[:, :, SPAN * g : SPAN * (g + 1)].rearrange("p a (m i t) -> p m a t i", t=PACK, i=16),
+            )
+            return ordered
+
         gather_words(0, 0)
         gather_words(1, 0)
-        w1_q[0, 0] = quantise(round_weight(w1_raw[0, 0], False), "w1_00")
+        v_planes = keep.tile([P, 2, S], U8, align_bytes=64)
+        for side in range(2):
+            nc.vector.tensor_copy(v_planes[:, side, :], tab_planes[:].indirect(lists[side][:]))
 
-        w_sorted = keep.tile([P, H], U8, align_bytes=64)
-        nc.vector.tensor_copy(
-            out=w_sorted[:].rearrange("p (g t m i) -> p g m t i", g=HP, t=PACK, i=16),
-            in_=w_planes[:].rearrange("p (g m i t) -> p g m t i", g=HP, t=PACK, i=16),
-        )
-        for n in range(1, KP + HP):
-            nc.gpsimd.dma_start(out=w_moved[n - 1][0:LIVE, :].bitcast(I32), in_=w_sorted[4 * n : 4 * n + LIVE, :].bitcast(I32))
-        w_scales = [w_sorted, *w_moved]
+        def move_v_plane(a):
+            nc.sync.dma_start(
+                out=v_moved[a - 1][0:LIVE, :, :].rearrange("p l s -> p (l s)").bitcast(I32),
+                in_=v_planes[4 * a : 4 * a + LIVE, :, :].rearrange("p l s -> p (l s)").bitcast(I32),
+            )
 
-        for a in range(1, KP):
-            gather_words(0, a)
-            gather_words(1, a)
-            w1_q[a, 0] = quantise(round_weight(w1_raw[a, 0], False), f"w1_{a}0")
-
-        w1_raw[1, 1] = load_float(w1, 1, 1)
-        w1_raw[2, 1] = load_float(w1, 2, 1)
-        w3_raw[0, 0] = load_float(w3, 0, 0)
+        move_v_plane(1)
+        w1_raw[2, 0] = load_float(w1, 2, 0, "raw2")
+        move_v_plane(2)
+        v_scales = [v_planes, *v_moved]
 
         def sort_w2(g):
             words = keep.tile([P, KP, SPAN], I32, align_bytes=64, name=f"w2_sorted{g}")
             nc.vector.tensor_copy(
-                out=words[:].rearrange("p a (t m i) -> p a m t i", t=PACK, i=4),
-                in_=w2_raw[g][:].rearrange("p a (m i t) -> p a m t i", t=PACK, i=4),
+                out=words[:].rearrange("p a (t m i) -> p m a t i", t=PACK, i=4),
+                in_=w2_raw[g][:].rearrange("p a (m i t) -> p m a t i", t=PACK, i=4),
             )
             return words
 
-        def first_product(tag, side, weight):
+        w1_q, w2_sorted, w2_ordered = {}, {}, {}
+        for a in range(KP):
+            if a > 0:
+                gather_words(0, a)
+                gather_words(1, a)
+            w1_q[a, 0] = quantise(round_weight(w1_raw[a, 0], C20 if a == 2 else 0, f"first{a}"), f"w1_{a}0")
+            if a == 0:
+                w2_sorted[0] = sort_w2(0)
+                w2_ordered[0] = sort_planes(w2_planes, 0, "w2_ordered0")
+        w1_raw[0, 1] = load_float(w1, 0, 1, "raw0")
+        w2_raw[1] = load_w2(1, "tab1")
+        w1_raw[1, 1] = load_float(w1, 1, 1, "raw1")
+        w1_raw[2, 1] = load_float(w1, 2, 1, "tab2")
+        w4_raw = keep.tile([P, HP, H], U16, align_bytes=64, name="raw2")
+        nc.sync.dma_start(out=w4_raw[:].bitcast(I32), in_=w4_words.rearrange("a p x -> p a x").bitcast(I32))
+        w2_ordered[1] = sort_planes(w2_planes, 1, "first2")
+        w2_sorted[1] = sort_w2(1)
+        w1_q[0, 1] = quantise(round_weight(w1_raw[0, 1], 0), "w1_01")
+        w3_raw[0, 0] = load_float(w3, 0, 0, "raw0")
+
+        def first_product(tag, side, weight, order):
             banks = [psum.tile([P, PACK, CHUNK], F32, name=f"{tag}{c}") for c in range(CHUNKS)]
-            for a in range(KP):
-                for c in range(CHUNKS):
+            for a, c in order:
+                for unit in range(1):
                     cols = slice(CHUNK * c, CHUNK * (c + 1))
                     for t in range(PACK):
                         codes, scales = weight(a, t)
@@ -169,35 +199,48 @@ def tile_list_syndicate_pair_features_kernel(
                         )
             return banks
 
-        h_q, lead = [], []
+        h_q, lead, w3_q = [], [], {}
         for g in range(HP):
-            w2_sorted = sort_w2(g)
-            if g == 0:
-                w4_raw = keep.tile([P, HP, H], U16, name="packed_raw0")
-                nc.sync.dma_start(out=w4_raw[:].bitcast(I32), in_=w4_words.rearrange("a p x -> p a x").bitcast(I32))
             if g == 1:
-                for a in range(KP):
-                    w1_q[a, 1] = quantise(round_weight(w1_raw[a, 1], a > 0), f"w1_{a}1")
-                w3_raw[1, 0] = load_float(w3, 1, 0)
-                w3_raw[0, 1] = load_float(w3, 0, 1)
-                w3_raw[1, 1] = load_float(w3, 1, 1)
+                for a in range(1, KP):
+                    w1_q[a, 1] = quantise(round_weight(w1_raw[a, 1], (0, C11, C21)[a], f"second{a}"), f"w1_{a}1")
+                w3_raw[1, 0] = load_float(w3, 1, 0, "tab1")
+                w3_raw[0, 1] = load_float(w3, 0, 1, "raw1")
+                w3_raw[1, 1] = load_float(w3, 1, 1, "tab2")
+                for a in range(HP):
+                    w3_q[a, 0] = quantise(round_weight(w3_raw[a, 0], (D00, D10)[a]), f"w3_{a}0")
 
             def w1_block(a, t):
                 codes, scales = w1_q[a, g]
                 return codes[:, P * t : P * (t + 1)], scales[:, P * t : P * (t + 1)]
 
             def w2_block(a, t):
-                first = SPAN * g + P * t
-                return w2_sorted[:, a, P * t : P * (t + 1)], w_scales[a][:, first : first + P]
+                return w2_sorted[g][:, a, P * t : P * (t + 1)], w2_ordered[g][:, a, P * t : P * (t + 1)]
 
+            by_pass = [(a, c) for a in range(KP) for c in range(CHUNKS)]
+            by_bank = [(a, c) for c in range(CHUNKS) for a in range(KP)]
             if g == 0:
-                p_banks = first_product("left", 0, w1_block)
-                b_banks = first_product("right", 1, w2_block)
+                p_banks = first_product("left", 0, w1_block, by_pass)
+                b_banks = first_product("right", 1, w2_block, by_pass)
             else:
-                b_banks = first_product("right", 1, w2_block)
-                p_banks = first_product("left", 0, w1_block)
-            h = keep.tile([P, PACK * S], BF16, align_bytes=64, name=f"h{g}")
-            p_rows = keep.tile([P, PACK, S], F32, name=f"p_rows{g}")
+                b_banks = first_product("right", 1, w2_block, by_bank)
+                p_banks = first_product("left", 0, w1_block, by_pass)
+            if g == 1:
+                w4_ordered = keep.tile([P, H], U8, align_bytes=64, name="second2")
+                nc.vector.tensor_copy(
+                    out=w4_ordered[:].rearrange("p (g t m i) -> p g m t i", g=HP, t=PACK, i=16),
+                    in_=w4_planes[:, 0, :].rearrange("p (g m i t) -> p g m t i", g=HP, t=PACK, i=16),
+                )
+                nc.gpsimd.dma_start(out=w4_moved[0:LIVE, :].bitcast(I32), in_=w4_ordered[4 : 4 + LIVE, :].bitcast(I32))
+                w4_scale = [w4_ordered, w4_moved]
+                w4_sorted = keep.tile([P, HP, H], U16, align_bytes=64, name="second1")
+                nc.vector.tensor_copy(
+                    out=w4_sorted[:].rearrange("p a (g t m i) -> p (a g) m t i", g=HP, t=PACK, i=8),
+                    in_=w4_raw[:].rearrange("p a (g m i t) -> p (a g) m t i", g=HP, t=PACK, i=8),
+                )
+            kept = PACK - AGAIN if g == AG else PACK
+            h = keep.tile([P, PACK * S], BF16, align_bytes=64, name=("tab1", "h1")[g])
+            p_rows = keep.tile([P, kept, S], F32, name=f"p_rows{g}")
             for c in range(CHUNKS):
                 gate = stage.tile([P, CHUNK, PACK], F32, name="gate")
                 nc.scalar.activation(out=gate[:], in_=p_banks[c][:].rearrange("p t n -> p n t"), func=ACT.Silu)
@@ -207,48 +250,60 @@ def tile_list_syndicate_pair_features_kernel(
                     in1=gate[:],
                     op=ALU.mult,
                 )
-            for c in range(CHUNKS):
-                nc.scalar.copy(out=p_rows[:, :, CHUNK * c : CHUNK * (c + 1)], in_=p_banks[c][:])
+                if g == 0 and WEAVE:
+                    nc.scalar.copy(out=p_rows[:, :, CHUNK * c : CHUNK * (c + 1)], in_=p_banks[c][:, 0:kept, :])
+            for c in range(0 if g == 0 and WEAVE else CHUNKS):
+                nc.scalar.copy(out=p_rows[:, :, CHUNK * c : CHUNK * (c + 1)], in_=p_banks[c][:, 0:kept, :])
             h_q.append(quantise(h, f"h{g}"))
             lead.append(p_rows)
-            if g == 0:
-                w4_sorted = keep.tile([P, HP, H], U16, align_bytes=64)
-                nc.vector.tensor_copy(
-                    out=w4_sorted[:].rearrange("p a (g t m i) -> p (a g) m t i", g=HP, t=PACK, i=8),
-                    in_=w4_raw[:].rearrange("p a (g m i t) -> p (a g) m t i", g=HP, t=PACK, i=8),
+
+        for a in range(HP):
+            w3_q[a, 1] = quantise(round_weight(w3_raw[a, 1], (D01, D11)[a]), f"w3_{a}1")
+        def accumulate(bank, passes):
+            for n, (codes, scales, moving, moving_scales) in enumerate(passes):
+                nc.tensor.matmul_mx(
+                    out=bank[:],
+                    lhsT=codes,
+                    lhsT_scale=scales,
+                    rhs=moving,
+                    rhs_scale=moving_scales,
+                    start=(n == 0),
+                    stop=(n == len(passes) - 1),
                 )
 
+        gated = [(codes[:].bitcast(FP8X4), scales[:]) for codes, scales in h_q]
         for g in range(HP):
-            w3_q = [quantise(round_weight(w3_raw[a, g], g == 0 and a == 0), f"w3_{a}{g}") for a in range(HP)]
             rows = out[SPAN * g : SPAN * (g + 1), :].rearrange("(p t) j -> p t j", t=PACK)
+            d_banks, y_banks, squashed = [], [], []
             for t in range(PACK):
-                first = SPAN * g + P * t
-                y_bank = psum.tile([P, S], F32, name=f"right{t}")
-                d_bank = psum.tile([P, S], F32, name=f"left{t}")
-                for a in range(HP):
-                    nc.tensor.matmul_mx(
-                        out=y_bank[:],
-                        lhsT=w4_sorted[:, a, first : first + P].bitcast(FP4X4),
-                        lhsT_scale=w_scales[KP + a][:, first : first + P],
-                        rhs=h_q[a][0][:].bitcast(FP8X4),
-                        rhs_scale=h_q[a][1][:],
-                        start=(a == 0),
-                        stop=(a == HP - 1),
-                    )
-                for a in range(HP):
-                    nc.tensor.matmul_mx(
-                        out=d_bank[:],
-                        lhsT=w3_q[a][0][:, P * t : P * (t + 1)].bitcast(FP8X4),
-                        lhsT_scale=w3_q[a][1][:, P * t : P * (t + 1)],
-                        rhs=h_q[a][0][:].bitcast(FP8X4),
-                        rhs_scale=h_q[a][1][:],
-                        start=(a == 0),
-                        stop=(a == HP - 1),
-                    )
-                inner = stage.tile([P, S], F32, name="inner")
-                nc.vector.tensor_tensor(out=inner[:], in0=d_bank[:], in1=lead[g][:, t, :], op=ALU.add)
-                squashed = stage.tile([P, S], F32, name="squashed")
-                nc.scalar.activation(out=squashed[:], in_=inner[:], func=ACT.Tanh)
-                result = stage.tile([P, S], F32, name="result")
-                nc.vector.tensor_tensor(out=result[:], in0=y_bank[:], in1=squashed[:], op=ALU.add)
+                block = slice(P * t, P * (t + 1))
+                passes = []
+                if t >= lead[g].shape[1]:
+                    passes = [
+                        (w1_q[a, g][0][:, block].bitcast(FP8X4), w1_q[a, g][1][:, block], v_words[0, a][:].bitcast(FP4X4), v_scales[a][:, 0, :])
+                        for a in range(KP)
+                    ]
+                passes = passes + [
+                    (w3_q[a, g][0][:, block].bitcast(FP8X4), w3_q[a, g][1][:, block], *gated[a]) for a in range(HP)
+                ]
+                d_banks.append(psum.tile([P, S], F32, name=f"right{t}"))
+                accumulate(d_banks[t], passes)
+            for t in range(PACK):
+                block = slice(SPAN * g + P * t, SPAN * g + P * (t + 1))
+                y_banks.append(psum.tile([P, S], F32, name=f"left{t}"))
+                accumulate(
+                    y_banks[t],
+                    [(w4_sorted[:, a, block].bitcast(FP4X4), w4_scale[a][:, block], *gated[a]) for a in range(HP)],
+                )
+            for t in range(PACK):
+                inner = d_banks[t]
+                if t < lead[g].shape[1]:
+                    inner = stage.tile([P, S], F32, name="inner")
+                    kept_row = lead[g][:, t, :]
+                    nc.vector.tensor_tensor(out=inner[:], in0=d_banks[t][:], in1=kept_row, op=ALU.add)
+                squashed.append(keep.tile([P, S], F32, name=f"squashed{g}{t}"))
+                nc.scalar.activation(out=squashed[t][:], in_=inner[:], func=ACT.Tanh)
+            for t in range(PACK):
+                result = keep.tile([P, S], F32, name=f"result{g}{t}")
+                nc.vector.tensor_tensor(out=result[:], in0=y_banks[t][:], in1=squashed[t][:], op=ALU.add)
                 nc.sync.dma_start(out=rows[:, t, :], in_=result[:])

@@ -26,6 +26,7 @@ CHUNKS = S // CHUNK
 LIVE = 100
 AGAIN = 2
 AG = 1
+LATE = "h1"
 WEAVE = False
 C20, C11, C21, D00, D10, D01, D11 = 0, 0, 4, 0, 4, 0, 0
 
@@ -62,11 +63,9 @@ def tile_list_syndicate_pair_features_kernel(
         nc.gpsimd.memset(tab_planes[:].bitcast(I32), 0)
         for tile in [w2_planes, *v_moved]:
             nc.vector.memset(tile[:].rearrange("p a c -> p (a c)").bitcast(I32), 0)
-        w4_planes = keep.tile([P, 1, H], U8, align_bytes=64)
-        w4_moved = keep.tile([P, H], U8, align_bytes=64)
-        for tile in [w4_planes[:, 0, :], w4_moved[:]]:
-            nc.vector.memset(tile.bitcast(I32), 0)
-        load_packed_planes(nc.gpsimd, w4_planes[:, 0, :], w4_scales)
+        w4_planes = keep.tile([P, HP, H], U8, align_bytes=64)
+        nc.vector.memset(w4_planes[:].rearrange("p a c -> p (a c)").bitcast(I32), 0)
+        load_planes(nc.gpsimd, w4_planes, w4_scales)
         warm = keep.tile([P, 2], F32)
         nc.vector.memset(warm[:], 0.0)
         nc.scalar.activation(out=warm[:, 1:2], in_=warm[:, 0:1], func=ACT.Silu)
@@ -105,12 +104,12 @@ def tile_list_syndicate_pair_features_kernel(
                 rounded = stage.tile([P, PACK * SPAN], BF16, align_bytes=64, name="rounded")
             else:
                 rounded = keep.tile([P, PACK * SPAN], BF16, align_bytes=64, name=slot)
-            dst = rounded[:].rearrange("p (t m j) -> p m j t", t=PACK, j=PACK)
-            src = raw[:].rearrange("p j (m t) -> p m j t", t=PACK)
-            if on_vector > 0:
-                nc.vector.tensor_copy(out=dst[:, :, :, 0:on_vector], in_=src[:, :, :, 0:on_vector])
-            if on_vector < PACK:
-                nc.scalar.copy(out=dst[:, :, :, on_vector:PACK], in_=src[:, :, :, on_vector:PACK])
+            dst = rounded[:].rearrange("p (u t m j) -> p u m j t", u=2, t=2, j=PACK)
+            src = raw[:].rearrange("p j (m u t) -> p u m j t", u=2, t=2)
+            if on_vector:
+                nc.vector.tensor_copy(out=dst, in_=src)
+            else:
+                nc.scalar.copy(out=dst, in_=src)
             return rounded
 
         def quantise(values, name):
@@ -226,13 +225,7 @@ def tile_list_syndicate_pair_features_kernel(
                 b_banks = first_product("right", 1, w2_block, by_bank)
                 p_banks = first_product("left", 0, w1_block, by_pass)
             if g == 1:
-                w4_ordered = keep.tile([P, H], U8, align_bytes=64, name="second2")
-                nc.vector.tensor_copy(
-                    out=w4_ordered[:].rearrange("p (g t m i) -> p g m t i", g=HP, t=PACK, i=16),
-                    in_=w4_planes[:, 0, :].rearrange("p (g m i t) -> p g m t i", g=HP, t=PACK, i=16),
-                )
-                nc.gpsimd.dma_start(out=w4_moved[0:LIVE, :].bitcast(I32), in_=w4_ordered[4 : 4 + LIVE, :].bitcast(I32))
-                w4_scale = [w4_ordered, w4_moved]
+                w4_ordered = [sort_planes(w4_planes, 0, "second2")]
                 w4_sorted = keep.tile([P, HP, H], U16, align_bytes=64, name="second1")
                 nc.vector.tensor_copy(
                     out=w4_sorted[:].rearrange("p a (g t m i) -> p (a g) m t i", g=HP, t=PACK, i=8),
@@ -259,6 +252,8 @@ def tile_list_syndicate_pair_features_kernel(
 
         for a in range(HP):
             w3_q[a, 1] = quantise(round_weight(w3_raw[a, 1], (D01, D11)[a]), f"w3_{a}1")
+        w4_ordered.append(sort_planes(w4_planes, 1, LATE))
+
         def accumulate(bank, passes):
             for n, (codes, scales, moving, moving_scales) in enumerate(passes):
                 nc.tensor.matmul_mx(
@@ -293,7 +288,7 @@ def tile_list_syndicate_pair_features_kernel(
                 y_banks.append(psum.tile([P, S], F32, name=f"left{t}"))
                 accumulate(
                     y_banks[t],
-                    [(w4_sorted[:, a, block].bitcast(FP4X4), w4_scale[a][:, block], *gated[a]) for a in range(HP)],
+                    [(w4_sorted[:, a, block].bitcast(FP4X4), w4_ordered[g][:, a, P * t : P * (t + 1)], *gated[a]) for a in range(HP)],
                 )
             for t in range(PACK):
                 inner = d_banks[t]

@@ -235,11 +235,13 @@ def tile_list_syndicate_pair_features_kernel(
             h = keep.tile([P, PACK * S], BF16, align_bytes=64, name=("tab1", "h1")[g])
             p_rows = keep.tile([P, kept, S], F32, name=f"p_rows{g}")
             for c in range(CHUNKS):
-                gate = stage.tile([P, CHUNK, PACK], F32, name="gate")
-                nc.scalar.activation(out=gate[:], in_=p_banks[c][:].rearrange("p t n -> p n t"), func=ACT.Silu)
+                gate = stage.tile([P, CHUNK // 2, PACK, 2], F32, name="gate")
+                nc.scalar.activation(
+                    out=gate[:], in_=p_banks[c][:].rearrange("p t (n i) -> p n t i", i=2), func=ACT.Silu
+                )
                 nc.vector.tensor_tensor(
-                    out=h[:, SPAN * c : SPAN * (c + 1)].rearrange("p (n t) -> p n t", t=PACK),
-                    in0=b_banks[c][:].rearrange("p t n -> p n t"),
+                    out=h[:, SPAN * c : SPAN * (c + 1)].rearrange("p (n i t) -> p n t i", i=2, t=PACK),
+                    in0=b_banks[c][:].rearrange("p t (n i) -> p n t i", i=2),
                     in1=gate[:],
                     op=ALU.mult,
                 )

@@ -19,16 +19,16 @@ ALU = mybir.AluOpType
 P = 128
 PACK = 4
 SPAN = P * PACK
-KP = K // SPAN
-HP = H // SPAN
+K_PASSES = K // SPAN
+HALVES = H // SPAN
+QUADRANTS = 4
+QUADRANT = 32
+LIVE = 4
+LAST_LIVE = QUADRANT * (QUADRANTS - 1) + LIVE
 CHUNK = 128
 CHUNKS = S // CHUNK
-LIVE = 100
-AGAIN = 2
-AG = 1
-LATE = "h1"
-WEAVE = False
-C20, C11, C21, D00, D10, D01, D11 = 0, 0, 4, 0, 4, 0, 0
+LEAD, STARTUP = 0, 1
+KEPT_IN_HALF_1 = 2
 
 
 def tile_list_syndicate_pair_features_kernel(
@@ -40,76 +40,72 @@ def tile_list_syndicate_pair_features_kernel(
         stage = ctx.enter_context(tc.tile_pool(name="stage", bufs=4))
         psum = ctx.enter_context(tc.psum_pool(name="psum", bufs=1))
 
-        lists = [keep.tile([P, S // 16], U16, name=f"list{i}") for i in range(2)]
-        tab_planes = keep.tile([P, T], U8, align_bytes=64, name="raw2")
-        w2_planes = keep.tile([P, KP, H], U8, align_bytes=64)
-        v_moved = [keep.tile([P, 2, S], U8, align_bytes=64, name=f"v_moved{i}") for i in range(KP - 1)]
-
-        def load_packed_planes(queue, tile, scales):
-            rows = 4 * scales.shape[0]
-            for q in range(4):
-                queue.dma_start(
-                    out=tile[32 * q : 32 * q + rows, :].bitcast(I32),
-                    in_=scales[:, 4 * q : 4 * q + 4, :].bitcast(I32),
-                )
-
-        def load_planes(queue, tile, scales):
-            for q in range(4):
-                queue.dma_start(
-                    out=tile[32 * q : 32 * q + 4, :, :].bitcast(I32),
-                    in_=scales[:, 4 * q : 4 * q + 4, :].rearrange("a r c -> r a c").bitcast(I32),
-                )
+        lists = [keep.tile([P, S // 16], U16, name=f"list{side}") for side in (LEAD, STARTUP)]
+        tab_planes = keep.tile([P, T], U8, align_bytes=64, name="buffer2")
+        weight_planes = keep.tile([P, K_PASSES, H], U8, align_bytes=64)
+        v_moved = [keep.tile([P, 2, S], U8, align_bytes=64, name=f"v_moved{a}") for a in range(1, K_PASSES)]
 
         nc.gpsimd.memset(tab_planes[:].bitcast(I32), 0)
-        for tile in [w2_planes, *v_moved]:
+        for tile in [weight_planes, *v_moved]:
             nc.vector.memset(tile[:].rearrange("p a c -> p (a c)").bitcast(I32), 0)
-        w4_planes = keep.tile([P, HP, H], U8, align_bytes=64)
-        nc.vector.memset(w4_planes[:].rearrange("p a c -> p (a c)").bitcast(I32), 0)
-        load_planes(nc.gpsimd, w4_planes, w4_scales)
         warm = keep.tile([P, 2], F32)
         nc.vector.memset(warm[:], 0.0)
         nc.scalar.activation(out=warm[:, 1:2], in_=warm[:, 0:1], func=ACT.Silu)
 
-        def load_float(w, a, g, slot):
-            raw = keep.tile([P, PACK, SPAN], F32, align_bytes=64, name=slot)
+        tab = [keep.tile([P, T], U16, align_bytes=64, name=f"table{a}") for a in range(K_PASSES)]
+
+        def load_tab_words(a):
+            nc.sync.dma_start(out=tab[a][:].bitcast(I32), in_=tab_words[a].bitcast(I32))
+
+        def load_tab_planes():
+            for q in range(QUADRANTS):
+                nc.sync.dma_start(
+                    out=tab_planes[QUADRANT * q : QUADRANT * q + LIVE * K_PASSES, :].bitcast(I32),
+                    in_=tab_scales[:, LIVE * q : LIVE * (q + 1), :].bitcast(I32),
+                )
+
+        def load_weight_planes(queue, planes, scales):
+            for q in range(QUADRANTS):
+                queue.dma_start(
+                    out=planes[QUADRANT * q : QUADRANT * q + LIVE, :, :].bitcast(I32),
+                    in_=scales[:, LIVE * q : LIVE * (q + 1), :].rearrange("a r c -> r a c").bitcast(I32),
+                )
+
+        def load_float(w, a, g, buffer):
+            raw = keep.tile([P, PACK, SPAN], F32, align_bytes=64, name=buffer)
             rows = w[SPAN * a : SPAN * (a + 1), SPAN * g : SPAN * (g + 1)]
             nc.sync.dma_start(out=raw[:], in_=rows.rearrange("(p j) c -> p j c", j=PACK))
             return raw
 
-        def load_w2(g, slot):
-            words = keep.tile([P, KP, SPAN], I32, align_bytes=64, name=slot)
+        def load_w2_words(g, buffer):
+            words = keep.tile([P, K_PASSES, SPAN], I32, align_bytes=64, name=buffer)
             cols = w2_words[:, :, SPAN * g : SPAN * (g + 1), :]
             nc.sync.dma_start(out=words[:], in_=cols.rearrange("a p c i -> p a (c i)").bitcast(I32))
             return words
 
-        tab = [keep.tile([P, T], U16, align_bytes=64, name=f"tab{a}") for a in range(KP)]
-        w1_raw, w2_raw, w3_raw = {}, {}, {}
+        def rounding_views(raw, rounded):
+            return (
+                rounded[:].rearrange("p (u e m j) -> p u m j e", u=2, e=2, j=PACK),
+                raw[:].rearrange("p j (m u e) -> p u m j e", u=2, e=2),
+            )
 
-        def load_tab(a):
-            nc.sync.dma_start(out=tab[a][:].bitcast(I32), in_=tab_words[a].bitcast(I32))
+        def round_on_scalar(raw, pool, buffer):
+            rounded = pool.tile([P, PACK * SPAN], BF16, align_bytes=64, name=buffer)
+            dst, src = rounding_views(raw, rounded)
+            nc.scalar.copy(out=dst, in_=src)
+            return rounded
 
-        nc.sync.dma_start(lists[0][:], offs)
-        nc.sync.dma_start(lists[1][:], offs2)
-        load_tab(0)
-        w1_raw[0, 0] = load_float(w1, 0, 0, "raw0")
-        load_packed_planes(nc.sync, tab_planes, tab_scales)
-        w2_raw[0] = load_w2(0, "w2_raw")
-        load_tab(1)
-        load_planes(nc.sync, w2_planes, w2_scales)
-        w1_raw[1, 0] = load_float(w1, 1, 0, "raw1")
-        load_tab(2)
+        def round_on_vector(raw, pool, buffer):
+            rounded = pool.tile([P, PACK * SPAN], BF16, align_bytes=64, name=buffer)
+            dst, src = rounding_views(raw, rounded)
+            nc.vector.tensor_copy(out=dst, in_=src)
+            return rounded
 
-        def round_weight(raw, on_vector, slot=None):
-            if slot is None:
-                rounded = stage.tile([P, PACK * SPAN], BF16, align_bytes=64, name="rounded")
-            else:
-                rounded = keep.tile([P, PACK * SPAN], BF16, align_bytes=64, name=slot)
-            dst = rounded[:].rearrange("p (u t m j) -> p u m j t", u=2, t=2, j=PACK)
-            src = raw[:].rearrange("p j (m u t) -> p u m j t", u=2, t=2)
-            if on_vector:
-                nc.vector.tensor_copy(out=dst, in_=src)
-            else:
-                nc.scalar.copy(out=dst, in_=src)
+        def round_on_both(raw, pool, buffer):
+            rounded = pool.tile([P, PACK * SPAN], BF16, align_bytes=64, name=buffer)
+            dst, src = rounding_views(raw, rounded)
+            nc.vector.tensor_copy(out=dst[:, 0], in_=src[:, 0])
+            nc.scalar.copy(out=dst[:, 1], in_=src[:, 1])
             return rounded
 
         def quantise(values, name):
@@ -120,120 +116,61 @@ def tile_list_syndicate_pair_features_kernel(
 
         v_words = {}
 
-        def gather_words(side, a):
-            slot = f"first{a - 1}" if side == 0 and a > 0 else f"v_words{side}{a}"
-            words = keep.tile([P, S], U16, align_bytes=64, name=slot)
+        def gather_words(side, a, buffer):
+            words = keep.tile([P, S], U16, align_bytes=64, name=buffer)
             nc.vector.tensor_copy(words[:], tab[a][:].indirect(lists[side][:]))
             v_words[side, a] = words
 
-        def sort_planes(planes, g, name):
-            passes = planes.shape[1]
-            ordered = keep.tile([P, passes, SPAN], U8, align_bytes=64, name=name)
+        def order_planes(planes, g, buffer):
+            ordered = keep.tile([P, planes.shape[1], SPAN], U8, align_bytes=64, name=buffer)
             nc.vector.tensor_copy(
-                out=ordered[:].rearrange("p a (t m i) -> p m a t i", t=PACK, i=16),
-                in_=planes[:, :, SPAN * g : SPAN * (g + 1)].rearrange("p a (m i t) -> p m a t i", t=PACK, i=16),
+                out=ordered[:].rearrange("p a (t n i) -> p n a t i", t=PACK, i=16),
+                in_=planes[:, :, SPAN * g : SPAN * (g + 1)].rearrange("p a (n i t) -> p n a t i", t=PACK, i=16),
             )
             return ordered
 
-        gather_words(0, 0)
-        gather_words(1, 0)
-        v_planes = keep.tile([P, 2, S], U8, align_bytes=64)
-        for side in range(2):
-            nc.vector.tensor_copy(v_planes[:, side, :], tab_planes[:].indirect(lists[side][:]))
+        def order_w2_words(words, g):
+            ordered = keep.tile([P, K_PASSES, SPAN], I32, align_bytes=64, name=f"w2_codes{g}")
+            nc.vector.tensor_copy(
+                out=ordered[:].rearrange("p a (t n i) -> p n a t i", t=PACK, i=4),
+                in_=words[:].rearrange("p a (n i t) -> p n a t i", t=PACK, i=4),
+            )
+            return ordered
+
+        def order_w4_words(words, buffer):
+            ordered = keep.tile([P, HALVES, H], U16, align_bytes=64, name=buffer)
+            nc.vector.tensor_copy(
+                out=ordered[:].rearrange("p a (g t n i) -> p (a g) n t i", g=HALVES, t=PACK, i=8),
+                in_=words[:].rearrange("p a (g n i t) -> p (a g) n t i", g=HALVES, t=PACK, i=8),
+            )
+            return ordered
 
         def move_v_plane(a):
             nc.sync.dma_start(
-                out=v_moved[a - 1][0:LIVE, :, :].rearrange("p l s -> p (l s)").bitcast(I32),
-                in_=v_planes[4 * a : 4 * a + LIVE, :, :].rearrange("p l s -> p (l s)").bitcast(I32),
+                out=v_moved[a - 1][0:LAST_LIVE, :, :].rearrange("p l s -> p (l s)").bitcast(I32),
+                in_=v_planes[LIVE * a : LIVE * a + LAST_LIVE, :, :].rearrange("p l s -> p (l s)").bitcast(I32),
             )
-
-        move_v_plane(1)
-        w1_raw[2, 0] = load_float(w1, 2, 0, "raw2")
-        move_v_plane(2)
-        v_scales = [v_planes, *v_moved]
-
-        def sort_w2(g):
-            words = keep.tile([P, KP, SPAN], I32, align_bytes=64, name=f"w2_sorted{g}")
-            nc.vector.tensor_copy(
-                out=words[:].rearrange("p a (t m i) -> p m a t i", t=PACK, i=4),
-                in_=w2_raw[g][:].rearrange("p a (m i t) -> p m a t i", t=PACK, i=4),
-            )
-            return words
-
-        w1_q, w2_sorted, w2_ordered = {}, {}, {}
-        for a in range(KP):
-            if a > 0:
-                gather_words(0, a)
-                gather_words(1, a)
-            w1_q[a, 0] = quantise(round_weight(w1_raw[a, 0], C20 if a == 2 else 0, f"first{a}"), f"w1_{a}0")
-            if a == 0:
-                w2_sorted[0] = sort_w2(0)
-                w2_ordered[0] = sort_planes(w2_planes, 0, "w2_ordered0")
-        w1_raw[0, 1] = load_float(w1, 0, 1, "raw0")
-        w2_raw[1] = load_w2(1, "tab1")
-        w1_raw[1, 1] = load_float(w1, 1, 1, "raw1")
-        w1_raw[2, 1] = load_float(w1, 2, 1, "tab2")
-        w4_raw = keep.tile([P, HP, H], U16, align_bytes=64, name="raw2")
-        nc.sync.dma_start(out=w4_raw[:].bitcast(I32), in_=w4_words.rearrange("a p x -> p a x").bitcast(I32))
-        w2_ordered[1] = sort_planes(w2_planes, 1, "first2")
-        w2_sorted[1] = sort_w2(1)
-        w1_q[0, 1] = quantise(round_weight(w1_raw[0, 1], 0), "w1_01")
-        w3_raw[0, 0] = load_float(w3, 0, 0, "raw0")
 
         def first_product(tag, side, weight, order):
             banks = [psum.tile([P, PACK, CHUNK], F32, name=f"{tag}{c}") for c in range(CHUNKS)]
             for a, c in order:
-                for unit in range(1):
-                    cols = slice(CHUNK * c, CHUNK * (c + 1))
-                    for t in range(PACK):
-                        codes, scales = weight(a, t)
-                        nc.tensor.matmul_mx(
-                            out=banks[c][:, t, :],
-                            lhsT=codes.bitcast(FP8X4),
-                            lhsT_scale=scales,
-                            rhs=v_words[side, a][:, cols].bitcast(FP4X4),
-                            rhs_scale=v_scales[a][:, side, cols],
-                            start=(a == 0 and t == 0),
-                            stop=(a == KP - 1 and t == PACK - 1),
-                        )
+                pairs = slice(CHUNK * c, CHUNK * (c + 1))
+                for t in range(PACK):
+                    places = slice(P * t, P * (t + 1))
+                    nc.tensor.matmul_mx(
+                        out=banks[c][:, t, :],
+                        lhsT=weight[a][0][:, places].bitcast(FP8X4),
+                        lhsT_scale=weight[a][1][:, places],
+                        rhs=v_words[side, a][:, pairs].bitcast(FP4X4),
+                        rhs_scale=v_scales[a][:, side, pairs],
+                        start=(a == 0 and t == 0),
+                        stop=(a == K_PASSES - 1 and t == PACK - 1),
+                    )
             return banks
 
-        h_q, lead, w3_q = [], [], {}
-        for g in range(HP):
-            if g == 1:
-                for a in range(1, KP):
-                    w1_q[a, 1] = quantise(round_weight(w1_raw[a, 1], (0, C11, C21)[a], f"second{a}"), f"w1_{a}1")
-                w3_raw[1, 0] = load_float(w3, 1, 0, "tab1")
-                w3_raw[0, 1] = load_float(w3, 0, 1, "raw1")
-                w3_raw[1, 1] = load_float(w3, 1, 1, "tab2")
-                for a in range(HP):
-                    w3_q[a, 0] = quantise(round_weight(w3_raw[a, 0], (D00, D10)[a]), f"w3_{a}0")
-
-            def w1_block(a, t):
-                codes, scales = w1_q[a, g]
-                return codes[:, P * t : P * (t + 1)], scales[:, P * t : P * (t + 1)]
-
-            def w2_block(a, t):
-                return w2_sorted[g][:, a, P * t : P * (t + 1)], w2_ordered[g][:, a, P * t : P * (t + 1)]
-
-            by_pass = [(a, c) for a in range(KP) for c in range(CHUNKS)]
-            by_bank = [(a, c) for c in range(CHUNKS) for a in range(KP)]
-            if g == 0:
-                p_banks = first_product("left", 0, w1_block, by_pass)
-                b_banks = first_product("right", 1, w2_block, by_pass)
-            else:
-                b_banks = first_product("right", 1, w2_block, by_bank)
-                p_banks = first_product("left", 0, w1_block, by_pass)
-            if g == 1:
-                w4_ordered = [sort_planes(w4_planes, 0, "second2")]
-                w4_sorted = keep.tile([P, HP, H], U16, align_bytes=64, name="second1")
-                nc.vector.tensor_copy(
-                    out=w4_sorted[:].rearrange("p a (g t m i) -> p (a g) m t i", g=HP, t=PACK, i=8),
-                    in_=w4_raw[:].rearrange("p a (g m i t) -> p (a g) m t i", g=HP, t=PACK, i=8),
-                )
-            kept = PACK - AGAIN if g == AG else PACK
-            h = keep.tile([P, PACK * S], BF16, align_bytes=64, name=("tab1", "h1")[g])
-            p_rows = keep.tile([P, kept, S], F32, name=f"p_rows{g}")
+        def gate_half(g, p_banks, b_banks, kept, buffer):
+            h = keep.tile([P, PACK * S], BF16, align_bytes=64, name=buffer)
+            p_rows = keep.tile([P, kept, S], F32, align_bytes=64, name=f"p_rows{g}")
             for c in range(CHUNKS):
                 gate = stage.tile([P, CHUNK // 2, PACK, 2], F32, name="gate")
                 nc.scalar.activation(
@@ -245,16 +182,9 @@ def tile_list_syndicate_pair_features_kernel(
                     in1=gate[:],
                     op=ALU.mult,
                 )
-                if g == 0 and WEAVE:
-                    nc.scalar.copy(out=p_rows[:, :, CHUNK * c : CHUNK * (c + 1)], in_=p_banks[c][:, 0:kept, :])
-            for c in range(0 if g == 0 and WEAVE else CHUNKS):
+            for c in range(CHUNKS):
                 nc.scalar.copy(out=p_rows[:, :, CHUNK * c : CHUNK * (c + 1)], in_=p_banks[c][:, 0:kept, :])
-            h_q.append(quantise(h, f"h{g}"))
-            lead.append(p_rows)
-
-        for a in range(HP):
-            w3_q[a, 1] = quantise(round_weight(w3_raw[a, 1], (D01, D11)[a]), f"w3_{a}1")
-        w4_ordered.append(sort_planes(w4_planes, 1, LATE))
+            return quantise(h, f"h{g}"), p_rows
 
         def accumulate(bank, passes):
             for n, (codes, scales, moving, moving_scales) in enumerate(passes):
@@ -268,39 +198,122 @@ def tile_list_syndicate_pair_features_kernel(
                     stop=(n == len(passes) - 1),
                 )
 
-        gated = [(codes[:].bitcast(FP8X4), scales[:]) for codes, scales in h_q]
-        for g in range(HP):
-            rows = out[SPAN * g : SPAN * (g + 1), :].rearrange("(p t) j -> p t j", t=PACK)
+        w1_raw, w1_q, w3_raw, w3_q = {}, {}, {}, {}
+        nc.sync.dma_start(lists[LEAD][:], offs)
+        nc.sync.dma_start(lists[STARTUP][:], offs2)
+        load_tab_words(0)
+        w1_raw[0, 0] = load_float(w1, 0, 0, "buffer0")
+        load_tab_planes()
+        w2_raw = load_w2_words(0, "w2_raw")
+        load_tab_words(1)
+        load_weight_planes(nc.sync, weight_planes, w2_scales)
+        w1_raw[1, 0] = load_float(w1, 1, 0, "buffer1")
+        load_tab_words(2)
+
+        gather_words(LEAD, 0, "lead_words0")
+        gather_words(STARTUP, 0, "startup_words0")
+        v_planes = keep.tile([P, 2, S], U8, align_bytes=64)
+        for side in (LEAD, STARTUP):
+            nc.vector.tensor_copy(v_planes[:, side, :], tab_planes[:].indirect(lists[side][:]))
+        move_v_plane(1)
+        w1_raw[2, 0] = load_float(w1, 2, 0, "buffer2")
+        move_v_plane(2)
+        v_scales = [v_planes, *v_moved]
+
+        w1_q[0, 0] = quantise(round_on_scalar(w1_raw[0, 0], keep, "handover0"), "w1_00")
+        w2_codes = [order_w2_words(w2_raw, 0)]
+        w2_planes = [order_planes(weight_planes, 0, "w2_planes0")]
+        gather_words(LEAD, 1, "handover0")
+        gather_words(STARTUP, 1, "startup_words1")
+        w1_q[1, 0] = quantise(round_on_scalar(w1_raw[1, 0], keep, "handover1"), "w1_10")
+        gather_words(LEAD, 2, "handover1")
+        gather_words(STARTUP, 2, "startup_words2")
+        w1_q[2, 0] = quantise(round_on_scalar(w1_raw[2, 0], keep, "handover2"), "w1_20")
+
+        w1_raw[0, 1] = load_float(w1, 0, 1, "buffer0")
+        w2_raw = load_w2_words(1, "table1")
+        w1_raw[1, 1] = load_float(w1, 1, 1, "buffer1")
+        w1_raw[2, 1] = load_float(w1, 2, 1, "table2")
+        w3_raw[0, 0] = load_float(w3, 0, 0, "buffer2")
+        w2_planes.append(order_planes(weight_planes, 1, "handover2"))
+        w4_raw_planes = weight_planes[:, 0:HALVES, :]
+        load_weight_planes(nc.gpsimd, w4_raw_planes, w4_scales)
+        w2_codes.append(order_w2_words(w2_raw, 1))
+        w1_q[0, 1] = quantise(round_on_scalar(w1_raw[0, 1], stage, "rounded"), "w1_01")
+        w3_raw[1, 0] = load_float(w3, 1, 0, "buffer0")
+
+        def w1_half(g):
+            return [w1_q[a, g] for a in range(K_PASSES)]
+
+        def w2_half(g):
+            return [(w2_codes[g][:, a, :], w2_planes[g][:, a, :]) for a in range(K_PASSES)]
+
+        by_pass = [(a, c) for a in range(K_PASSES) for c in range(CHUNKS)]
+        p_banks = first_product("left", LEAD, w1_half(0), by_pass)
+        b_banks = first_product("right", STARTUP, w2_half(0), by_pass)
+        h_first, p_first = gate_half(0, p_banks, b_banks, PACK, "table1")
+
+        w1_q[1, 1] = quantise(round_on_scalar(w1_raw[1, 1], keep, "handover3"), "w1_11")
+        w1_q[2, 1] = quantise(round_on_vector(w1_raw[2, 1], keep, "handover4"), "w1_21")
+        w4_raw = keep.tile([P, HALVES, H], U16, align_bytes=64, name="table1")
+        nc.sync.dma_start(out=w4_raw[:].bitcast(I32), in_=w4_words.rearrange("a p x -> p a x").bitcast(I32))
+        w3_raw[0, 1] = load_float(w3, 0, 1, "buffer1")
+        w3_raw[1, 1] = load_float(w3, 1, 1, "table2")
+        w3_q[0, 0] = quantise(round_on_scalar(w3_raw[0, 0], stage, "rounded"), "w3_00")
+        w3_q[1, 0] = quantise(round_on_both(w3_raw[1, 0], stage, "rounded"), "w3_10")
+
+        by_bank = [(a, c) for c in range(CHUNKS) for a in range(K_PASSES)]
+        b_banks = first_product("right", STARTUP, w2_half(1), by_bank)
+        p_banks = first_product("left", LEAD, w1_half(1), by_pass)
+        w4_planes = [order_planes(w4_raw_planes, 0, "handover4"), order_planes(w4_raw_planes, 1, "handover3")]
+        h_second, p_second = gate_half(1, p_banks, b_banks, KEPT_IN_HALF_1, "h_second")
+
+        for a in range(HALVES):
+            w3_q[a, 1] = quantise(round_on_scalar(w3_raw[a, 1], stage, "rounded"), f"w3_{a}1")
+        w4_codes = order_w4_words(w4_raw, "h_second")
+
+        gated = [(codes[:].bitcast(FP8X4), scales[:]) for codes, scales in (h_first, h_second)]
+        looked_up = [(v_words[LEAD, a][:].bitcast(FP4X4), v_scales[a][:, LEAD, :]) for a in range(K_PASSES)]
+
+        def cascade(g, p_rows):
+            kept = p_rows.shape[1]
             d_banks, y_banks, squashed = [], [], []
             for t in range(PACK):
-                block = slice(P * t, P * (t + 1))
-                passes = []
-                if t >= lead[g].shape[1]:
-                    passes = [
-                        (w1_q[a, g][0][:, block].bitcast(FP8X4), w1_q[a, g][1][:, block], v_words[0, a][:].bitcast(FP4X4), v_scales[a][:, 0, :])
-                        for a in range(KP)
-                    ]
-                passes = passes + [
-                    (w3_q[a, g][0][:, block].bitcast(FP8X4), w3_q[a, g][1][:, block], *gated[a]) for a in range(HP)
-                ]
+                places = slice(P * t, P * (t + 1))
+                operands = [(w3_q[a, g], gated[a]) for a in range(HALVES)]
+                if t >= kept:
+                    operands = [(w1_q[a, g], looked_up[a]) for a in range(K_PASSES)] + operands
                 d_banks.append(psum.tile([P, S], F32, name=f"right{t}"))
-                accumulate(d_banks[t], passes)
+                accumulate(
+                    d_banks[t],
+                    [(w[0][:, places].bitcast(FP8X4), w[1][:, places], *moving) for w, moving in operands],
+                )
             for t in range(PACK):
-                block = slice(SPAN * g + P * t, SPAN * g + P * (t + 1))
+                places = slice(P * t, P * (t + 1))
+                columns = slice(SPAN * g + P * t, SPAN * g + P * (t + 1))
                 y_banks.append(psum.tile([P, S], F32, name=f"left{t}"))
                 accumulate(
                     y_banks[t],
-                    [(w4_sorted[:, a, block].bitcast(FP4X4), w4_ordered[g][:, a, P * t : P * (t + 1)], *gated[a]) for a in range(HP)],
+                    [
+                        (w4_codes[:, a, columns].bitcast(FP4X4), w4_planes[g][:, a, places], *gated[a])
+                        for a in range(HALVES)
+                    ],
                 )
             for t in range(PACK):
                 inner = d_banks[t]
-                if t < lead[g].shape[1]:
+                if t < kept:
                     inner = stage.tile([P, S], F32, name="inner")
-                    kept_row = lead[g][:, t, :]
-                    nc.vector.tensor_tensor(out=inner[:], in0=d_banks[t][:], in1=kept_row, op=ALU.add)
+                    nc.vector.tensor_tensor(out=inner[:], in0=d_banks[t][:], in1=p_rows[:, t, :], op=ALU.add)
                 squashed.append(keep.tile([P, S], F32, name=f"squashed{g}{t}"))
                 nc.scalar.activation(out=squashed[t][:], in_=inner[:], func=ACT.Tanh)
+            return squashed, y_banks
+
+        def finish(g, squashed, y_banks):
+            rows = out[SPAN * g : SPAN * (g + 1), :].rearrange("(p t) j -> p t j", t=PACK)
             for t in range(PACK):
                 result = keep.tile([P, S], F32, name=f"result{g}{t}")
                 nc.vector.tensor_tensor(out=result[:], in0=y_banks[t][:], in1=squashed[t][:], op=ALU.add)
                 nc.sync.dma_start(out=rows[:, t, :], in_=result[:])
+
+        for g, p_rows in enumerate((p_first, p_second)):
+            finish(g, *cascade(g, p_rows))

from contextlib import ExitStack

import concourse.mybir as mybir

K, T, S, H = 1536, 2048, 512, 1024
FLOPS = 2 * S * H * (2 * K + 2 * H)

F32 = mybir.dt.float32
BF16 = mybir.dt.bfloat16
I32 = mybir.dt.int32
U32 = mybir.dt.uint32
U16 = mybir.dt.uint16
U8 = mybir.dt.uint8
FP8X4 = mybir.dt.float8_e4m3fn_x4
FP4X4 = mybir.dt.float4_e2m1fn_x4
ACT = mybir.ActivationFunctionType
ALU = mybir.AluOpType

P = 128
PACK = 4
SPAN = P * PACK
K_PASSES = K // SPAN
HALVES = H // SPAN
QUADRANTS = 4
QUADRANT = 32
LIVE = 4
LAST_LIVE = QUADRANT * (QUADRANTS - 1) + LIVE
CHUNK = 128
CHUNKS = S // CHUNK
LEAD, STARTUP = 0, 1
KEPT_IN_HALF_1 = 2


def tile_list_syndicate_pair_features_kernel(
    tc, tab_words, tab_scales, offs, offs2, w1, w2_words, w2_scales, w3, w4_words, w4_scales, out
):
    nc = tc.nc
    with ExitStack() as ctx:
        keep = ctx.enter_context(tc.tile_pool(name="keep", bufs=1))
        stage = ctx.enter_context(tc.tile_pool(name="stage", bufs=4))
        psum = ctx.enter_context(tc.psum_pool(name="psum", bufs=1))

        lists = [keep.tile([P, S // 16], U16, name=f"list{side}") for side in (LEAD, STARTUP)]
        tab_planes = keep.tile([P, T], U8, align_bytes=64, name="buffer2")
        weight_planes = keep.tile([P, K_PASSES, H], U8, align_bytes=64)
        v_moved = [keep.tile([P, 2, S], U8, align_bytes=64, name=f"v_moved{a}") for a in range(1, K_PASSES)]

        nc.gpsimd.memset(tab_planes[:].bitcast(I32), 0)
        for tile in [weight_planes, *v_moved]:
            nc.vector.memset(tile[:].rearrange("p a c -> p (a c)").bitcast(I32), 0)
        warm = keep.tile([P, 2], F32)
        nc.vector.memset(warm[:], 0.0)
        nc.scalar.activation(out=warm[:, 1:2], in_=warm[:, 0:1], func=ACT.Silu)

        tab = [keep.tile([P, T], U16, align_bytes=64, name=f"table{a}") for a in range(K_PASSES)]

        def load_tab_words(a):
            nc.sync.dma_start(out=tab[a][:].bitcast(I32), in_=tab_words[a].bitcast(I32))

        def load_tab_planes():
            for q in range(QUADRANTS):
                nc.sync.dma_start(
                    out=tab_planes[QUADRANT * q : QUADRANT * q + LIVE * K_PASSES, :].bitcast(I32),
                    in_=tab_scales[:, LIVE * q : LIVE * (q + 1), :].bitcast(I32),
                )

        def load_weight_planes(queue, planes, scales):
            for q in range(QUADRANTS):
                queue.dma_start(
                    out=planes[QUADRANT * q : QUADRANT * q + LIVE, :, :].bitcast(I32),
                    in_=scales[:, LIVE * q : LIVE * (q + 1), :].rearrange("a r c -> r a c").bitcast(I32),
                )

        def load_float(w, a, g, buffer):
            raw = keep.tile([P, PACK, SPAN], F32, align_bytes=64, name=buffer)
            rows = w[SPAN * a : SPAN * (a + 1), SPAN * g : SPAN * (g + 1)]
            nc.sync.dma_start(out=raw[:], in_=rows.rearrange("(p j) c -> p j c", j=PACK))
            return raw

        def load_w2_words(g, buffer):
            words = keep.tile([P, K_PASSES, SPAN], I32, align_bytes=64, name=buffer)
            cols = w2_words[:, :, SPAN * g : SPAN * (g + 1), :]
            nc.sync.dma_start(out=words[:], in_=cols.rearrange("a p c i -> p a (c i)").bitcast(I32))
            return words

        def rounding_views(raw, rounded):
            return (
                rounded[:].rearrange("p (u e m j) -> p u m j e", u=2, e=2, j=PACK),
                raw[:].rearrange("p j (m u e) -> p u m j e", u=2, e=2),
            )

        def round_on_scalar(raw, pool, buffer):
            rounded = pool.tile([P, PACK * SPAN], BF16, align_bytes=64, name=buffer)
            dst, src = rounding_views(raw, rounded)
            nc.scalar.copy(out=dst, in_=src)
            return rounded

        def round_on_vector(raw, pool, buffer):
            rounded = pool.tile([P, PACK * SPAN], BF16, align_bytes=64, name=buffer)
            dst, src = rounding_views(raw, rounded)
            nc.vector.tensor_copy(out=dst, in_=src)
            return rounded

        def round_on_both(raw, pool, buffer):
            rounded = pool.tile([P, PACK * SPAN], BF16, align_bytes=64, name=buffer)
            dst, src = rounding_views(raw, rounded)
            nc.vector.tensor_copy(out=dst[:, 0], in_=src[:, 0])
            nc.scalar.copy(out=dst[:, 1], in_=src[:, 1])
            return rounded

        def quantise(values, name):
            codes = keep.tile([P, SPAN], U32, align_bytes=64, name=f"{name}_codes")
            scales = keep.tile([P, SPAN], U8, align_bytes=64, name=f"{name}_scales")
            nc.vector.quantize_mx(out=codes[:].bitcast(FP8X4), scales=scales[:], in_=values[:])
            return codes, scales

        v_words = {}

        def gather_words(side, a, buffer):
            words = keep.tile([P, S], U16, align_bytes=64, name=buffer)
            nc.vector.tensor_copy(words[:], tab[a][:].indirect(lists[side][:]))
            v_words[side, a] = words

        def order_planes(planes, g, buffer):
            ordered = keep.tile([P, planes.shape[1], SPAN], U8, align_bytes=64, name=buffer)
            nc.vector.tensor_copy(
                out=ordered[:].rearrange("p a (t n i) -> p n a t i", t=PACK, i=16),
                in_=planes[:, :, SPAN * g : SPAN * (g + 1)].rearrange("p a (n i t) -> p n a t i", t=PACK, i=16),
            )
            return ordered

        def order_w2_words(words, g):
            ordered = keep.tile([P, K_PASSES, SPAN], I32, align_bytes=64, name=f"w2_codes{g}")
            nc.vector.tensor_copy(
                out=ordered[:].rearrange("p a (t n i) -> p n a t i", t=PACK, i=4),
                in_=words[:].rearrange("p a (n i t) -> p n a t i", t=PACK, i=4),
            )
            return ordered

        def order_w4_words(words, buffer):
            ordered = keep.tile([P, HALVES, H], U16, align_bytes=64, name=buffer)
            nc.vector.tensor_copy(
                out=ordered[:].rearrange("p a (g t n i) -> p (a g) n t i", g=HALVES, t=PACK, i=8),
                in_=words[:].rearrange("p a (g n i t) -> p (a g) n t i", g=HALVES, t=PACK, i=8),
            )
            return ordered

        def move_v_plane(a):
            nc.sync.dma_start(
                out=v_moved[a - 1][0:LAST_LIVE, :, :].rearrange("p l s -> p (l s)").bitcast(I32),
                in_=v_planes[LIVE * a : LIVE * a + LAST_LIVE, :, :].rearrange("p l s -> p (l s)").bitcast(I32),
            )

        def first_product(tag, side, weight, order):
            banks = [psum.tile([P, PACK, CHUNK], F32, name=f"{tag}{c}") for c in range(CHUNKS)]
            for a, c in order:
                pairs = slice(CHUNK * c, CHUNK * (c + 1))
                for t in range(PACK):
                    places = slice(P * t, P * (t + 1))
                    nc.tensor.matmul_mx(
                        out=banks[c][:, t, :],
                        lhsT=weight[a][0][:, places].bitcast(FP8X4),
                        lhsT_scale=weight[a][1][:, places],
                        rhs=v_words[side, a][:, pairs].bitcast(FP4X4),
                        rhs_scale=v_scales[a][:, side, pairs],
                        start=(a == 0 and t == 0),
                        stop=(a == K_PASSES - 1 and t == PACK - 1),
                    )
            return banks

        def gate_half(g, p_banks, b_banks, kept, buffer):
            h = keep.tile([P, PACK * S], BF16, align_bytes=64, name=buffer)
            p_rows = keep.tile([P, kept, S], F32, align_bytes=64, name=f"p_rows{g}")
            for c in range(CHUNKS):
                gate = stage.tile([P, CHUNK // 2, PACK, 2], F32, name="gate")
                nc.scalar.activation(
                    out=gate[:], in_=p_banks[c][:].rearrange("p t (n i) -> p n t i", i=2), func=ACT.Silu
                )
                nc.vector.tensor_tensor(
                    out=h[:, SPAN * c : SPAN * (c + 1)].rearrange("p (n i t) -> p n t i", i=2, t=PACK),
                    in0=b_banks[c][:].rearrange("p t (n i) -> p n t i", i=2),
                    in1=gate[:],
                    op=ALU.mult,
                )
            for c in range(CHUNKS):
                nc.scalar.copy(out=p_rows[:, :, CHUNK * c : CHUNK * (c + 1)], in_=p_banks[c][:, 0:kept, :])
            return quantise(h, f"h{g}"), p_rows

        def accumulate(bank, passes):
            for n, (codes, scales, moving, moving_scales) in enumerate(passes):
                nc.tensor.matmul_mx(
                    out=bank[:],
                    lhsT=codes,
                    lhsT_scale=scales,
                    rhs=moving,
                    rhs_scale=moving_scales,
                    start=(n == 0),
                    stop=(n == len(passes) - 1),
                )

        w1_raw, w1_q, w3_raw, w3_q = {}, {}, {}, {}
        nc.sync.dma_start(lists[LEAD][:], offs)
        nc.sync.dma_start(lists[STARTUP][:], offs2)
        load_tab_words(0)
        w1_raw[0, 0] = load_float(w1, 0, 0, "buffer0")
        load_tab_planes()
        w2_raw = load_w2_words(0, "w2_raw")
        load_tab_words(1)
        load_weight_planes(nc.sync, weight_planes, w2_scales)
        w1_raw[1, 0] = load_float(w1, 1, 0, "buffer1")
        load_tab_words(2)

        gather_words(LEAD, 0, "lead_words0")
        gather_words(STARTUP, 0, "startup_words0")
        v_planes = keep.tile([P, 2, S], U8, align_bytes=64)
        for side in (LEAD, STARTUP):
            nc.vector.tensor_copy(v_planes[:, side, :], tab_planes[:].indirect(lists[side][:]))
        move_v_plane(1)
        w1_raw[2, 0] = load_float(w1, 2, 0, "buffer2")
        move_v_plane(2)
        v_scales = [v_planes, *v_moved]

        w1_q[0, 0] = quantise(round_on_scalar(w1_raw[0, 0], keep, "handover0"), "w1_00")
        w2_codes = [order_w2_words(w2_raw, 0)]
        w2_planes = [order_planes(weight_planes, 0, "w2_planes0")]
        gather_words(LEAD, 1, "handover0")
        gather_words(STARTUP, 1, "startup_words1")
        w1_q[1, 0] = quantise(round_on_scalar(w1_raw[1, 0], keep, "handover1"), "w1_10")
        gather_words(LEAD, 2, "handover1")
        gather_words(STARTUP, 2, "startup_words2")
        w1_q[2, 0] = quantise(round_on_scalar(w1_raw[2, 0], keep, "handover2"), "w1_20")

        w1_raw[0, 1] = load_float(w1, 0, 1, "buffer0")
        w2_raw = load_w2_words(1, "table1")
        w1_raw[1, 1] = load_float(w1, 1, 1, "buffer1")
        w1_raw[2, 1] = load_float(w1, 2, 1, "table2")
        w3_raw[0, 0] = load_float(w3, 0, 0, "buffer2")
        w2_planes.append(order_planes(weight_planes, 1, "handover2"))
        w4_raw_planes = weight_planes[:, 0:HALVES, :]
        load_weight_planes(nc.gpsimd, w4_raw_planes, w4_scales)
        w2_codes.append(order_w2_words(w2_raw, 1))
        w1_q[0, 1] = quantise(round_on_scalar(w1_raw[0, 1], stage, "rounded"), "w1_01")
        w3_raw[1, 0] = load_float(w3, 1, 0, "buffer0")

        def w1_half(g):
            return [w1_q[a, g] for a in range(K_PASSES)]

        def w2_half(g):
            return [(w2_codes[g][:, a, :], w2_planes[g][:, a, :]) for a in range(K_PASSES)]

        by_pass = [(a, c) for a in range(K_PASSES) for c in range(CHUNKS)]
        p_banks = first_product("left", LEAD, w1_half(0), by_pass)
        b_banks = first_product("right", STARTUP, w2_half(0), by_pass)
        h_first, p_first = gate_half(0, p_banks, b_banks, PACK, "table1")

        w1_q[1, 1] = quantise(round_on_scalar(w1_raw[1, 1], keep, "handover3"), "w1_11")
        w1_q[2, 1] = quantise(round_on_vector(w1_raw[2, 1], keep, "handover4"), "w1_21")
        w4_raw = keep.tile([P, HALVES, H], U16, align_bytes=64, name="table1")
        nc.sync.dma_start(out=w4_raw[:].bitcast(I32), in_=w4_words.rearrange("a p x -> p a x").bitcast(I32))
        w3_raw[0, 1] = load_float(w3, 0, 1, "buffer1")
        w3_raw[1, 1] = load_float(w3, 1, 1, "table2")
        w3_q[0, 0] = quantise(round_on_scalar(w3_raw[0, 0], stage, "rounded"), "w3_00")
        w3_q[1, 0] = quantise(round_on_both(w3_raw[1, 0], stage, "rounded"), "w3_10")

        by_bank = [(a, c) for c in range(CHUNKS) for a in range(K_PASSES)]
        b_banks = first_product("right", STARTUP, w2_half(1), by_bank)
        p_banks = first_product("left", LEAD, w1_half(1), by_pass)
        w4_planes = [order_planes(w4_raw_planes, 0, "handover4"), order_planes(w4_raw_planes, 1, "handover3")]
        h_second, p_second = gate_half(1, p_banks, b_banks, KEPT_IN_HALF_1, "h_second")

        for a in range(HALVES):
            w3_q[a, 1] = quantise(round_on_scalar(w3_raw[a, 1], stage, "rounded"), f"w3_{a}1")
        w4_codes = order_w4_words(w4_raw, "h_second")

        gated = [(codes[:].bitcast(FP8X4), scales[:]) for codes, scales in (h_first, h_second)]
        looked_up = [(v_words[LEAD, a][:].bitcast(FP4X4), v_scales[a][:, LEAD, :]) for a in range(K_PASSES)]

        def cascade(g, p_rows):
            kept = p_rows.shape[1]
            d_banks, y_banks, squashed = [], [], []
            for t in range(PACK):
                places = slice(P * t, P * (t + 1))
                operands = [(w3_q[a, g], gated[a]) for a in range(HALVES)]
                if t >= kept:
                    operands = [(w1_q[a, g], looked_up[a]) for a in range(K_PASSES)] + operands
                d_banks.append(psum.tile([P, S], F32, name=f"right{t}"))
                accumulate(
                    d_banks[t],
                    [(w[0][:, places].bitcast(FP8X4), w[1][:, places], *moving) for w, moving in operands],
                )
            for t in range(PACK):
                places = slice(P * t, P * (t + 1))
                columns = slice(SPAN * g + P * t, SPAN * g + P * (t + 1))
                y_banks.append(psum.tile([P, S], F32, name=f"left{t}"))
                accumulate(
                    y_banks[t],
                    [
                        (w4_codes[:, a, columns].bitcast(FP4X4), w4_planes[g][:, a, places], *gated[a])
                        for a in range(HALVES)
                    ],
                )
            for t in range(PACK):
                inner = d_banks[t]
                if t < kept:
                    inner = stage.tile([P, S], F32, name="inner")
                    nc.vector.tensor_tensor(out=inner[:], in0=d_banks[t][:], in1=p_rows[:, t, :], op=ALU.add)
                squashed.append(keep.tile([P, S], F32, name=f"squashed{g}{t}"))
                nc.scalar.activation(out=squashed[t][:], in_=inner[:], func=ACT.Tanh)
            return squashed, y_banks

        def finish(g, squashed, y_banks):
            rows = out[SPAN * g : SPAN * (g + 1), :].rearrange("(p t) j -> p t j", t=PACK)
            for t in range(PACK):
                result = keep.tile([P, S], F32, name=f"result{g}{t}")
                nc.vector.tensor_tensor(out=result[:], in0=y_banks[t][:], in1=squashed[t][:], op=ALU.add)
                nc.sync.dma_start(out=rows[:, t, :], in_=result[:])

        for g, p_rows in enumerate((p_first, p_second)):
            finish(g, *cascade(g, p_rows))
